import numpy as np
import ml_dtypes


def mxq(x, axis, fmt="e4m3"):
    dtype, down = {"e4m3": (ml_dtypes.float8_e4m3fn, 7), "e5m2": (ml_dtypes.float8_e5m2, 14)}[fmt]
    v = np.moveaxis(np.asarray(x, np.float32).astype(ml_dtypes.bfloat16).astype(np.float64), axis, -1)
    blocks = v.reshape(v.shape[:-1] + (-1, 32))
    amax = np.abs(blocks).max(-1, keepdims=True)
    byte = np.maximum(np.where(amax > 0, np.frexp(amax)[1] - 1 + 127, 0) - down, 1)
    scale = np.exp2(byte - 127.0)
    codes = (blocks / scale).astype(np.float32).astype(dtype).astype(np.float64)
    return np.moveaxis((codes * scale).reshape(v.shape), -1, axis)


WIDE = False


def mx_kscale(k):
    if not WIDE:
        return np.ones(k)
    levels = np.array([10, -10, 5, -5, 0])
    if k % 512:
        return np.exp2(np.random.permutation(np.resize(levels, k // 32))).repeat(32)
    a = np.empty((k // 512, 16))
    for p in range(k // 512):
        a[p, :8] = np.random.permutation(np.resize(levels, 8))
        for g in range(8):
            far = levels[np.abs(levels - a[p, g]) >= 10]
            a[p, g + 8] = far[np.random.randint(len(far))]
    return np.exp2(a.ravel()).repeat(32)


BF16 = ml_dtypes.bfloat16


def bf(x):
    return np.asarray(x, np.float32).astype(BF16)


def f64(x):
    return np.asarray(x).astype(np.float64)


E2M1 = np.array([0.0, 0.5, 1.0, 1.5, 2.0, 3.0, 4.0, 6.0, -0.0, -0.5, -1.0, -1.5, -2.0, -3.0, -4.0, -6.0])


def pack_weight(w, fmt):
    k, n = w.shape
    w = f64(bf(w)).reshape(k // 32, 32, n)
    amax = np.abs(w).max(1)
    if fmt == "e4m3":
        byte = np.frexp(amax)[1] - 1 + 127 - 7
    else:
        mant, ex = np.frexp(amax / 6.0)
        byte = np.where(mant > 0.5, ex, ex - 1) + 127
    byte = np.clip(np.where(amax > 0, byte, 1), 1, 254)
    scaled = (w * np.exp2(127.0 - byte)[:, None, :]).reshape(k, n).astype(np.float32)
    by_word = np.ascontiguousarray(scaled.reshape(k // 512, 128, 4, n).transpose(0, 1, 3, 2))
    if fmt == "e4m3":
        words = by_word.astype(ml_dtypes.float8_e4m3fn).view(np.uint8)
    else:
        c = by_word.astype(ml_dtypes.float4_e2m1fn).view(np.uint8) & 0xF
        words = c[..., 0::2] | (c[..., 1::2] << 4)
    return np.ascontiguousarray(words), np.ascontiguousarray(byte.astype(np.uint8).reshape(k // 512, 16, n))


def unpack_weight(words, scales, fmt):
    g, p, n, _ = words.shape
    if fmt == "e4m3":
        vals = np.ascontiguousarray(words).view(ml_dtypes.float8_e4m3fn).astype(np.float64)
    else:
        nib = np.empty((g, p, n, 4), np.uint8)
        nib[..., 0::2] = words & 0xF
        nib[..., 1::2] = words >> 4
        vals = E2M1[nib]
    vals = vals * np.repeat(np.exp2(scales.astype(np.float64) - 127.0), 8, axis=1)[..., None]
    return vals.transpose(0, 1, 3, 2).reshape(g * 512, n)
def pack4(w):
    words, scales = pack_weight(w, "e2m1")
    return words.reshape(words.shape[0], 128, -1), scales


def unpack4(words, scales):
    return unpack_weight(words.reshape(words.shape[0], 128, -1, 2), scales, "e2m1")


def planes(Y):
    n, m = Y.shape
    b = f64(bf(Y)).reshape(n // 32, 32, m)
    amax = np.abs(b).max(1)
    byte = np.clip(np.where(amax > 0, np.frexp(amax)[1] - 1 + 127 - 7, 1), 1, 254)
    codes = (b * np.exp2(127.0 - byte)[:, None, :]).reshape(n, m).astype(np.float32).astype(ml_dtypes.float8_e4m3fn).view(np.uint8)
    words = codes.reshape(n // 512, 128, 4, m).transpose(0, 1, 3, 2)
    return np.ascontiguousarray(words), np.ascontiguousarray(byte.astype(np.uint8).reshape(n // 512, 16, m))


G, R, D, F = 4, 512, 1024, 512


def setup_inputs():
    s, t = mx_kscale(D), mx_kscale(F)
    spread = np.exp(0.8 * np.random.randn(G, D))
    z = np.random.randn(G, R, D) * s
    u = spread / s
    d = np.exp(0.4 * np.random.randn(G, F)) * t
    c = 0.3 * np.random.randn(G, D) * spread
    B = 1.2 * np.random.randn(G, D, F) / np.sqrt(D) / s[:, None]
    A = 1.2 * np.random.randn(G, F, D) / np.sqrt(F) * spread[:, None, :] / t[:, None]
    b_words, b_scales = pack4(B.reshape(G * D, F))
    a_words, a_scales = pack4(A.reshape(G * F, D))
    return {"z": bf(z), "u": bf(u), "d": bf(d), "c": bf(c),
            "b_words": b_words, "b_scales": b_scales,
            "a_words": a_words, "a_scales": a_scales}


def reference(z, u, d, c, b_words, b_scales, a_words, a_scales):
    z = f64(z)
    B = unpack4(b_words, b_scales).reshape(G, D, F)
    A = unpack4(a_words, a_scales).reshape(G, F, D)
    pre = mxq(z, 2, "e4m3") @ B
    h = np.tanh(pre) * f64(d)[:, None, :]
    o = mxq(h, 2, "e4m3") @ A
    y = f64(u)[:, None, :] * z + o + f64(c)[:, None, :]
    Y = y.reshape(G * R, D).T
    words, scales = planes(Y)
    return y, words, scales

@@ -1,0 +1,325 @@
+from contextlib import ExitStack
+
+import concourse.mybir as mybir
+from concourse.masks import make_identity
+
+G, R, D, F = 4, 512, 1024, 512
+FLOPS = 2 * G * R * D * F * 2
+
+F32 = mybir.dt.float32
+BF16 = mybir.dt.bfloat16
+I32 = mybir.dt.int32
+U32 = mybir.dt.uint32
+U8 = mybir.dt.uint8
+FP8X4 = mybir.dt.float8_e4m3fn_x4
+FP4X4 = mybir.dt.float4_e2m1fn_x4
+ACT = mybir.ActivationFunctionType
+ALU = mybir.AluOpType
+
+P = 128
+TILES = G * R // P
+PER_FLOW = R // P
+U_ROW, C_ROW, D_ROW, ROWS = 0, 8, 16, 20
+
+STEP = [('zT', -2, 0), ('zcopy', -2, 0), ('yq', 5, 1), ('add', 2, 0), ('add', 2, 1), ('hT', 1, 0), ('dmul', 1, 0), ('wTr', 1, 0), ('yT', 3, 0), ('wTr', 1, 1), ('castV', 2, 0), ('wcopy', 1, 0), ('wcopy', 1, 1), ('hq', 1, 0), ('mx1', 0, 0), ('mx2', 1, 0), ('zq', -1, 0), ('mx2', 1, 1), ('tanh', 0, 0), ('wTA', -1, (1, 5)), ('castV', 2, 1), ('ycopy', 3, 0), ('wTV', -1, (3, 7)), ('wTV', -1, (2, 6)), ('wTA', -1, (0, 4)), ('yq', 4, 0)]
+
+
+def tile_grouped_sylvester_step_k7_kernel(
+    tc, z, u, d, c, b_words, b_scales, a_words, a_scales, out_0, out_1, out_2
+):
+    nc = tc.nc
+    z_rows = z.rearrange("e r k -> (e r) k")
+    y_rows = out_0.rearrange("e r k -> (e r) k")
+
+    with ExitStack() as ctx:
+        keep = ctx.enter_context(tc.tile_pool(name="keep", bufs=1))
+        work = ctx.enter_context(tc.tile_pool(name="work", bufs=3))
+        psum = ctx.enter_context(tc.psum_pool(name="psum", bufs=1))
+        ctx.enter_context(tc.manual_schedule())
+
+        ident = keep.tile([P, P], F32, name="ident")
+        par_rows = keep.tile([P, 512], BF16, name="par_rows")
+        par = keep.tile([P, ROWS, 4], F32, name="par")
+        warm = keep.tile([P, 8], F32, name="warm")
+        b_plane = keep.tile([P, 2 * G, F], U8, name="b_plane", align_bytes=64)
+        a_plane = keep.tile([P, G, D], U8, name="a_plane", align_bytes=64)
+        z_raw = [keep.tile([P, D], BF16, name="z_raw%d" % i, align_bytes=64) for i in range(TILES)]
+        b_code = [keep.tile([P, 2, 2 * F], U8, name="b_code%d" % e, align_bytes=64) for e in range(G)]
+        a_code = [keep.tile([P, 2 * D], U8, name="a_code%d" % e, align_bytes=64) for e in range(G)]
+
+        def load_z(i):
+            nc.sync.dma_start(out=z_raw[i][:], in_=z_rows[P * i : P * (i + 1), :])
+
+        def load_b(e):
+            nc.sync.dma_start(
+                out=b_code[e][:].bitcast(I32),
+                in_=b_words[2 * e : 2 * e + 2].rearrange("g p n -> p g n").bitcast(I32),
+            )
+
+        def load_a(e):
+            nc.sync.dma_start(out=a_code[e][:].bitcast(I32), in_=a_words[e].bitcast(I32))
+
+        def load_plane(queue, plane, rows, first, last):
+            for q in range(4):
+                queue.dma_start(
+                    out=plane[32 * q : 32 * q + 4, first:last, :].bitcast(I32),
+                    in_=rows[first:last, 4 * q : 4 * q + 4, :].rearrange("g r n -> r g n").bitcast(I32),
+                )
+
+        make_identity(nc, ident[:])
+        nc.vector.memset(b_plane[:, 0:2, :].bitcast(I32), 0)
+        nc.vector.memset(par_rows[:], 0.0)
+        nc.vector.memset(a_plane[:, 0:1, :].bitcast(I32), 0)
+        nc.vector.memset(b_plane[:, 2:, :].bitcast(I32), 0)
+        nc.vector.memset(a_plane[:, 1:, :].bitcast(I32), 0)
+        load_z(0)
+        load_plane(nc.scalar, b_plane, b_scales, 0, 2)
+        nc.scalar.activation(out=warm[:], in_=ident[:, 0:8], func=ACT.Tanh)
+        load_b(0)
+        load_z(1)
+        nc.sync.dma_start(out=par_rows[U_ROW:C_ROW, :], in_=u.rearrange("e (g k) -> (e g) k", g=2))
+        nc.sync.dma_start(out=par_rows[C_ROW:D_ROW, :], in_=c.rearrange("e (g k) -> (e g) k", g=2))
+        nc.sync.dma_start(out=par_rows[D_ROW:ROWS, :], in_=d)
+        load_z(2)
+        load_plane(nc.sync, a_plane, a_scales, 0, 1)
+        load_a(0)
+        load_z(3)
+        load_z(4)
+        load_plane(nc.sync, b_plane, b_scales, 2, 2 * G)
+        load_plane(nc.sync, a_plane, a_scales, 1, G)
+        for e in range(1, G):
+            load_b(e)
+            load_a(e)
+            for i in range(PER_FLOW * e + 1, min(PER_FLOW * (e + 1) + 1, TILES)):
+                load_z(i)
+
+        t = {}
+
+        def spread_parameters():
+            bank = psum.tile([P, 4, P], F32, name="par_bank", tag="h_bank")
+            words = par_rows[:].bitcast(F32)
+            for half in range(2):
+                nc.tensor.transpose(bank[:, half, :], words[:, half:256:2], ident[:])
+            pairs = bank[:, 0:2, :].bitcast(BF16).rearrange("p h (j e) -> p j h e", e=2)
+            nc.vector.tensor_copy(out=par[:].rearrange("p j (h e) -> p j h e", e=2), in_=pairs[:, 0:ROWS])
+
+        def z_turn(i, g):
+            bank = psum.tile([P, 4, P], F32, name="z_bank", tag="z_bank")
+            words = z_raw[i][:].bitcast(F32)
+            for j in range(4):
+                first = 256 * (j // 2) + j % 2
+                nc.tensor.transpose(bank[:, j, :], words[:, first : 256 * (j // 2 + 1) : 2], ident[:])
+            t["z_bank", i] = bank
+            if i == 1:
+                spread_parameters()
+
+        def z_copy(i, copy):
+            if i % 2 == 0:
+                t["z_t", i // 2] = work.tile([P, 2, D], BF16, name="z_t", tag="z_t", align_bytes=64)
+            copy(
+                out=t["z_t", i // 2][:, i % 2, :].bitcast(F32).rearrange("p (g r h) -> p g r h", g=2, h=2),
+                in_=t["z_bank", i][:].rearrange("p (g h) r -> p g r h", g=2),
+            )
+
+        def z_quantise(i, g):
+            codes = work.tile([P, 2 * P], U32, name="z_codes", tag="z_codes", align_bytes=64)
+            scales = work.tile([P, 2 * P], U8, name="z_scales", tag="z_scales", align_bytes=64)
+            nc.vector.quantize_mx(out=codes[:].bitcast(FP8X4), scales=scales[:], in_=t["z_t", i // 2][:, i % 2, :])
+            t["z_mx", i] = (codes, scales)
+
+        def w_operands(pair, j):
+            if ("w_t", pair, j // 4) not in t:
+                t["w_t", pair, j // 4] = work.tile([P, 4, 2, P], F32, name="w_t", tag="w_t%d" % (j // 4))
+            row = 2 * (2 * pair // PER_FLOW) + j // 4
+            src = t["z_t", pair][:].rearrange("p i (g r t) -> p g t i r", g=2, t=4)[:, j // 4, j % 4]
+            return (
+                t["w_t", pair, j // 4][:, j % 4],
+                src,
+                par[:, U_ROW + row, j % 4 : j % 4 + 1],
+                par[:, C_ROW + row, j % 4 : j % 4 + 1],
+            )
+
+        def w_vector(pair, j):
+            dst, src, scale, shift = w_operands(pair, j)
+            nc.vector.tensor_scalar(out=dst, in0=src, scalar1=scale, scalar2=shift, op0=ALU.mult, op1=ALU.add)
+
+        def w_gpsimd(pair, j):
+            dst, src, scale, shift = w_operands(pair, j)
+            nc.gpsimd.tensor_scalar(out=dst, in0=src, scalar1=scale, scalar2=shift, op0=ALU.mult, op1=ALU.add)
+
+        def w_scalar(pair, j):
+            dst, src, scale, shift = w_operands(pair, j)
+            nc.scalar.activation(out=dst, in_=src, func=ACT.Identity, bias=shift, scale=scale)
+
+        def mx_first(i, g):
+            e = i // PER_FLOW
+            bank = psum.tile([P, F], F32, name="pre_bank", tag="pre_bank")
+            codes, scales = t["z_mx", i]
+            for k in range(2):
+                nc.tensor.matmul_mx(
+                    out=bank[:],
+                    lhsT=codes[:, P * k : P * (k + 1)].bitcast(FP8X4),
+                    lhsT_scale=scales[:, P * k : P * (k + 1)],
+                    rhs=b_code[e][:, k, :].bitcast(FP4X4),
+                    rhs_scale=b_plane[:, 2 * e + k, :],
+                    start=(k == 0),
+                    stop=(k == 1),
+                )
+            t["pre", i] = bank
+
+        def tanh(i, g):
+            th = work.tile([P, 4, P], F32, name="th", tag="th")
+            nc.scalar.activation(out=th[:], in_=t["pre", i][:].rearrange("r (m t) -> r t m", t=4), func=ACT.Tanh)
+            t["th", i] = th
+
+        def h_turn(i, g):
+            bank = psum.tile([P, 4, P], F32, name="h_bank", tag="h_bank")
+            for j in range(4):
+                nc.tensor.transpose(bank[:, j, :], t["th", i][:, j, :], ident[:])
+            t["h_bank", i] = bank
+
+        def h_scale(i, g):
+            h_t = work.tile([P, P, 4], BF16, name="h_t", tag="h_t", align_bytes=64)
+            gain = par[:, D_ROW + i // PER_FLOW, :].unsqueeze(1).to_broadcast([P, P, 4])
+            nc.vector.tensor_tensor(
+                out=h_t[:], in0=t["h_bank", i][:].rearrange("p t r -> p r t"), in1=gain, op=ALU.mult
+            )
+            t["h_t", i] = h_t
+
+        def h_quantise(i, g):
+            codes = work.tile([P, P], U32, name="h_codes", tag="h_codes", align_bytes=64)
+            scales = work.tile([P, P], U8, name="h_scales", tag="h_scales", align_bytes=64)
+            nc.vector.quantize_mx(
+                out=codes[:].bitcast(FP8X4), scales=scales[:], in_=t["h_t", i][:].rearrange("p r t -> p (r t)")
+            )
+            t["h_mx", i] = (codes, scales)
+
+        def w_turn(i, g):
+            bank = psum.tile([P, 4, P], F32, name="w_bank", tag="w_bank%d" % g)
+            for j in range(4):
+                nc.tensor.transpose(bank[:, j, :], t["w_t", i // 2, g][:, j, i % 2, :], ident[:])
+            t["w_bank", i, g] = bank
+
+        def w_copy(i, g):
+            w = work.tile([P, P, 4], F32, name="w", tag="w%d" % g)
+            nc.scalar.copy(out=w[:], in_=t["w_bank", i, g][:].rearrange("r t m -> r m t"))
+            t["w", i, g] = w
+
+        def mx_second(i, g):
+            e = i // PER_FLOW
+            bank = psum.tile([P, 512], F32, name="o_bank", tag="o_bank%d" % g)
+            codes, scales = t["h_mx", i]
+            nc.tensor.matmul_mx(
+                out=bank[:],
+                lhsT=codes[:].bitcast(FP8X4),
+                lhsT_scale=scales[:],
+                rhs=a_code[e][:, 1024 * g : 1024 * (g + 1)].bitcast(FP4X4),
+                rhs_scale=a_plane[:, e, 512 * g : 512 * (g + 1)],
+                start=True,
+                stop=True,
+            )
+            t["o", i, g] = bank
+
+        def add(i, g):
+            if ("y", i) not in t:
+                t["y", i] = work.tile([P, D], F32, name="y", tag="y", bufs=4)
+            nc.vector.tensor_tensor(
+                out=t["y", i][:, 512 * g : 512 * (g + 1)],
+                in0=t["o", i, g][:],
+                in1=t["w", i, g][:].rearrange("r m t -> r (m t)"),
+                op=ALU.add,
+            )
+            t["added", i] = t.get(("added", i), 0) + 1
+            if t["added", i] == 2:
+                nc.sync.dma_start(out=y_rows[P * i : P * (i + 1), :], in_=t["y", i][:])
+
+        def cast_operands(i, g):
+            y_b = work.tile([P, 2, P, 2], BF16, name="y_b", tag="y_b%d" % g)
+            t["y_b", i, g] = y_b
+            return y_b[:], t["y", i][:, 512 * g : 512 * (g + 1)].rearrange("r (p h e) -> r h p e", h=2, e=2)
+
+        def cast_vector(i, g):
+            dst, src = cast_operands(i, g)
+            nc.vector.tensor_copy(out=dst, in_=src)
+
+        def cast_scalar(i, g):
+            dst, src = cast_operands(i, g)
+            nc.scalar.copy(out=dst, in_=src)
+
+        def cast_gpsimd(i, g):
+            dst, src = cast_operands(i, g)
+            nc.gpsimd.tensor_scalar(out=dst, in0=src, scalar1=1.0, scalar2=0.0, op0=ALU.mult, op1=ALU.add)
+
+        def y_turn(i, g):
+            bank = psum.tile([P, 4, P], F32, name="y_bank", tag="y_bank")
+            for j in range(4):
+                words = t["y_b", i, j // 2][:].rearrange("r h p e -> r (h p e)").bitcast(F32)
+                nc.tensor.transpose(bank[:, j, :], words[:, P * (j % 2) : P * (j % 2 + 1)], ident[:])
+            t["y_bank", i] = bank
+
+        def y_copy(i, copy):
+            y_t = work.tile([P, D], BF16, name="y_t", tag="y_t", align_bytes=64, bufs=4)
+            copy(
+                out=y_t[:].bitcast(F32).rearrange("p (g r h) -> p g r h", g=2, h=2),
+                in_=t["y_bank", i][:].rearrange("p (g h) r -> p g r h", g=2),
+            )
+            t["y_t", i] = y_t
+
+        def y_quantise(i, g):
+            e, r0 = i // PER_FLOW, P * (i % PER_FLOW)
+            if ("y_mx", e) not in t:
+                codes = work.tile([P, 2, R], U32, name="y_codes", tag="y_codes", align_bytes=64, bufs=2)
+                scales = work.tile([P, 2, R], U8, name="y_scales", tag="y_scales", align_bytes=64, bufs=2)
+                t["y_mx", e] = (codes, scales)
+            codes, scales = t["y_mx", e]
+            nc.vector.quantize_mx(
+                out=codes[:, g, r0 : r0 + P].bitcast(FP8X4),
+                scales=scales[:, g, r0 : r0 + P],
+                in_=t["y_t", i][:, 512 * g : 512 * (g + 1)],
+            )
+            t["made", i // 2] = t.get(("made", i // 2), 0) + 1
+            if t["made", i // 2] == 4:
+                m0 = 2 * P * (i // 2)
+                nc.sync.dma_start(
+                    out=out_1[:, :, m0 : m0 + 2 * P, :].rearrange("g p m t -> p g (m t)").bitcast(I32),
+                    in_=codes[:, :, m0 % R : m0 % R + 2 * P].bitcast(I32),
+                )
+                if (i // 2) % 2 == 1:
+                    for q in range(4):
+                        nc.sync.dma_start(
+                            out=out_2[:, 4 * q : 4 * q + 4, R * e : R * (e + 1)].rearrange("g q m -> q g m").bitcast(I32),
+                            in_=scales[32 * q : 32 * q + 4, :, :].bitcast(I32),
+                        )
+
+        stage = {
+            "zT": z_turn,
+            "zcopy": lambda i, g: z_copy(i, nc.scalar.copy),
+            "zcopyV": lambda i, g: z_copy(i, nc.vector.tensor_copy),
+            "zq": z_quantise,
+            "mx1": mx_first,
+            "tanh": tanh,
+            "hT": h_turn,
+            "dmul": h_scale,
+            "hq": h_quantise,
+            "wTr": w_turn,
+            "wcopy": w_copy,
+            "mx2": mx_second,
+            "add": add,
+            "castV": cast_vector,
+            "castA": cast_scalar,
+            "castP": cast_gpsimd,
+            "yT": y_turn,
+            "ycopy": lambda i, g: y_copy(i, nc.scalar.copy),
+            "ycopyV": lambda i, g: y_copy(i, nc.vector.tensor_copy),
+            "yq": y_quantise,
+        }
+        pair_stage = {"wTV": w_vector, "wTA": w_scalar, "wTP": w_gpsimd}
+        lags = [lag for name, lag, g in STEP]
+        for s in range(min(lags), TILES + max(lags)):
+            for name, lag, g in STEP:
+                i = s - lag
+                if 0 <= i < TILES:
+                    if name in pair_stage:
+                        pair_stage[name](i // 2, g[i % 2])
+                    else:
+                        stage[name](i, g)

@@ -21,7 +21,40 @@ TILES = G * R // P
 PER_FLOW = R // P
 U_ROW, C_ROW, D_ROW, ROWS = 0, 8, 16, 20
 
-STEP = [('zT', -2, 0), ('zcopy', -2, 0), ('yq', 5, 1), ('add', 2, 0), ('add', 2, 1), ('hT', 1, 0), ('dmul', 1, 0), ('wTr', 1, 0), ('yT', 3, 0), ('wTr', 1, 1), ('castV', 2, 0), ('wcopy', 1, 0), ('wcopy', 1, 1), ('hq', 1, 0), ('mx1', 0, 0), ('mx2', 1, 0), ('zq', -1, 0), ('mx2', 1, 1), ('tanh', 0, 0), ('wTA', -1, (1, 5)), ('castV', 2, 1), ('ycopy', 3, 0), ('wTV', -1, (3, 7)), ('wTV', -1, (2, 6)), ('wTA', -1, (0, 4)), ('yq', 4, 0)]
+GROUP = 2
+STEP = [
+    ("mx1", "tensor", 2, 0),
+    ("wT", "scalar", 3, (5, 2)),
+    ("wT", "gpsimd", 5, (1, 3)),
+    ("zT", "tensor", 0, 0),
+    ("wT", "gpsimd", 3, (0, 4)),
+    ("wTr", "tensor", 6, 0),
+    ("tanh", "scalar", 2, 0),
+    ("cast", "gpsimd", 7, 1),
+    ("hq", "vector", 4, 0),
+    ("wTr", "tensor", 5, 1),
+    ("hT", "tensor", 3, 0),
+    ("zcopy", "scalar", 0, 0),
+    ("yT", "tensor", 8, 0),
+    ("mx2", "tensor", 6, 0),
+    ("mx2", "tensor", 5, 1),
+    ("wcopy", "scalar", 6, 0),
+    ("wcopy", "scalar", 5, 1),
+    ("dmul", "vector", 3, 0),
+    ("add", "vector", 6, 0),
+    ("ycopy", "scalar", 8, 0),
+    ("add", "vector", 5, 1),
+    ("cast", "vector", 6, 0),
+    ("wT", "gpsimd", 3, (6, 7)),
+    ("zq", "vector", 0, 0),
+    ("yq", "vector", 11, 0),
+]
+
+
+def depth(first, last, per=1):
+    lags_first = [lag for name, engine, lag, g in STEP if name == first]
+    lags_last = [lag for name, engine, lag, g in STEP if name == last]
+    return (max(lags_last) - min(lags_first) + per) // per + 2
 
 
 def tile_grouped_sylvester_step_k7_kernel(
@@ -103,7 +136,7 @@ def tile_grouped_sylvester_step_k7_kernel(
             pairs = bank[:, 0:2, :].bitcast(BF16).rearrange("p h (j e) -> p j h e", e=2)
             nc.vector.tensor_copy(out=par[:].rearrange("p j (h e) -> p j h e", e=2), in_=pairs[:, 0:ROWS])
 
-        def z_turn(i, g):
+        def z_turn(i, g, engine):
             bank = psum.tile([P, 4, P], F32, name="z_bank", tag="z_bank")
             words = z_raw[i][:].bitcast(F32)
             for j in range(4):
@@ -113,45 +146,51 @@ def tile_grouped_sylvester_step_k7_kernel(
             if i == 1:
                 spread_parameters()
 
-        def z_copy(i, copy):
-            if i % 2 == 0:
-                t["z_t", i // 2] = work.tile([P, 2, D], BF16, name="z_t", tag="z_t", align_bytes=64)
+        def copy(engine, out, in_):
+            if engine == "scalar":
+                nc.scalar.copy(out=out, in_=in_)
+            else:
+                nc.vector.tensor_copy(out=out, in_=in_)
+
+        def z_copy(i, g, engine):
+            if i % GROUP == 0:
+                t["z_t", i // GROUP] = work.tile(
+                    [P, GROUP, D], BF16, name="z_t", tag="z_t", align_bytes=64,
+                    bufs=max(depth("zcopy", "wT", GROUP), depth("zcopy", "zq", GROUP)),
+                )
             copy(
-                out=t["z_t", i // 2][:, i % 2, :].bitcast(F32).rearrange("p (g r h) -> p g r h", g=2, h=2),
-                in_=t["z_bank", i][:].rearrange("p (g h) r -> p g r h", g=2),
+                engine,
+                t["z_t", i // GROUP][:, i % GROUP, :].bitcast(F32).rearrange("p (g r h) -> p g r h", g=2, h=2),
+                t["z_bank", i][:].rearrange("p (g h) r -> p g r h", g=2),
             )
 
-        def z_quantise(i, g):
-            codes = work.tile([P, 2 * P], U32, name="z_codes", tag="z_codes", align_bytes=64)
-            scales = work.tile([P, 2 * P], U8, name="z_scales", tag="z_scales", align_bytes=64)
-            nc.vector.quantize_mx(out=codes[:].bitcast(FP8X4), scales=scales[:], in_=t["z_t", i // 2][:, i % 2, :])
+        def z_quantise(i, g, engine):
+            bufs = depth("zq", "mx1")
+            codes = work.tile([P, 2 * P], U32, name="z_codes", tag="z_codes", align_bytes=64, bufs=bufs)
+            scales = work.tile([P, 2 * P], U8, name="z_scales", tag="z_scales", align_bytes=64, bufs=bufs)
+            nc.vector.quantize_mx(
+                out=codes[:].bitcast(FP8X4), scales=scales[:], in_=t["z_t", i // GROUP][:, i % GROUP, :]
+            )
             t["z_mx", i] = (codes, scales)
 
-        def w_operands(pair, j):
-            if ("w_t", pair, j // 4) not in t:
-                t["w_t", pair, j // 4] = work.tile([P, 4, 2, P], F32, name="w_t", tag="w_t%d" % (j // 4))
-            row = 2 * (2 * pair // PER_FLOW) + j // 4
-            src = t["z_t", pair][:].rearrange("p i (g r t) -> p g t i r", g=2, t=4)[:, j // 4, j % 4]
-            return (
-                t["w_t", pair, j // 4][:, j % 4],
-                src,
-                par[:, U_ROW + row, j % 4 : j % 4 + 1],
-                par[:, C_ROW + row, j % 4 : j % 4 + 1],
-            )
+        def w_make(i, js, engine):
+            group, j = i // GROUP, js[i % GROUP]
+            if ("w_t", group, j // 4) not in t:
+                t["w_t", group, j // 4] = work.tile(
+                    [P, 4, GROUP, P], F32, name="w_t", tag="w_t%d" % (j // 4), bufs=depth("wT", "wTr", GROUP)
+                )
+            row = 2 * (i // PER_FLOW) + j // 4
+            dst = t["w_t", group, j // 4][:, j % 4]
+            src = t["z_t", group][:].rearrange("p i (g r t) -> p g t i r", g=2, t=4)[:, j // 4, j % 4]
+            scale = par[:, U_ROW + row, j % 4 : j % 4 + 1]
+            shift = par[:, C_ROW + row, j % 4 : j % 4 + 1]
+            if engine == "scalar":
+                nc.scalar.activation(out=dst, in_=src, func=ACT.Identity, bias=shift, scale=scale)
+            else:
+                unit = nc.vector if engine == "vector" else nc.gpsimd
+                unit.tensor_scalar(out=dst, in0=src, scalar1=scale, scalar2=shift, op0=ALU.mult, op1=ALU.add)
 
-        def w_vector(pair, j):
-            dst, src, scale, shift = w_operands(pair, j)
-            nc.vector.tensor_scalar(out=dst, in0=src, scalar1=scale, scalar2=shift, op0=ALU.mult, op1=ALU.add)
-
-        def w_gpsimd(pair, j):
-            dst, src, scale, shift = w_operands(pair, j)
-            nc.gpsimd.tensor_scalar(out=dst, in0=src, scalar1=scale, scalar2=shift, op0=ALU.mult, op1=ALU.add)
-
-        def w_scalar(pair, j):
-            dst, src, scale, shift = w_operands(pair, j)
-            nc.scalar.activation(out=dst, in_=src, func=ACT.Identity, bias=shift, scale=scale)
-
-        def mx_first(i, g):
+        def mx_first(i, g, engine):
             e = i // PER_FLOW
             bank = psum.tile([P, F], F32, name="pre_bank", tag="pre_bank")
             codes, scales = t["z_mx", i]
@@ -167,45 +206,45 @@ def tile_grouped_sylvester_step_k7_kernel(
                 )
             t["pre", i] = bank
 
-        def tanh(i, g):
-            th = work.tile([P, 4, P], F32, name="th", tag="th")
+        def tanh(i, g, engine):
+            th = work.tile([P, 4, P], F32, name="th", tag="th", bufs=depth("tanh", "hT"))
             nc.scalar.activation(out=th[:], in_=t["pre", i][:].rearrange("r (m t) -> r t m", t=4), func=ACT.Tanh)
             t["th", i] = th
 
-        def h_turn(i, g):
+        def h_turn(i, g, engine):
             bank = psum.tile([P, 4, P], F32, name="h_bank", tag="h_bank")
             for j in range(4):
                 nc.tensor.transpose(bank[:, j, :], t["th", i][:, j, :], ident[:])
             t["h_bank", i] = bank
 
-        def h_scale(i, g):
-            h_t = work.tile([P, P, 4], BF16, name="h_t", tag="h_t", align_bytes=64)
+        def h_scale(i, g, engine):
+            h_t = work.tile([P, P, 4], BF16, name="h_t", tag="h_t", align_bytes=64, bufs=depth("dmul", "hq"))
             gain = par[:, D_ROW + i // PER_FLOW, :].unsqueeze(1).to_broadcast([P, P, 4])
             nc.vector.tensor_tensor(
                 out=h_t[:], in0=t["h_bank", i][:].rearrange("p t r -> p r t"), in1=gain, op=ALU.mult
             )
             t["h_t", i] = h_t
 
-        def h_quantise(i, g):
-            codes = work.tile([P, P], U32, name="h_codes", tag="h_codes", align_bytes=64)
-            scales = work.tile([P, P], U8, name="h_scales", tag="h_scales", align_bytes=64)
+        def h_quantise(i, g, engine):
+            codes = work.tile([P, P], U32, name="h_codes", tag="h_codes", align_bytes=64, bufs=depth("hq", "mx2"))
+            scales = work.tile([P, P], U8, name="h_scales", tag="h_scales", align_bytes=64, bufs=depth("hq", "mx2"))
             nc.vector.quantize_mx(
                 out=codes[:].bitcast(FP8X4), scales=scales[:], in_=t["h_t", i][:].rearrange("p r t -> p (r t)")
             )
             t["h_mx", i] = (codes, scales)
 
-        def w_turn(i, g):
+        def w_turn(i, g, engine):
             bank = psum.tile([P, 4, P], F32, name="w_bank", tag="w_bank%d" % g)
             for j in range(4):
-                nc.tensor.transpose(bank[:, j, :], t["w_t", i // 2, g][:, j, i % 2, :], ident[:])
+                nc.tensor.transpose(bank[:, j, :], t["w_t", i // GROUP, g][:, j, i % GROUP, :], ident[:])
             t["w_bank", i, g] = bank
 
-        def w_copy(i, g):
-            w = work.tile([P, P, 4], F32, name="w", tag="w%d" % g)
-            nc.scalar.copy(out=w[:], in_=t["w_bank", i, g][:].rearrange("r t m -> r m t"))
+        def w_copy(i, g, engine):
+            w = work.tile([P, P, 4], F32, name="w", tag="w%d" % g, bufs=depth("wcopy", "add"))
+            copy(engine, w[:], t["w_bank", i, g][:].rearrange("r t m -> r m t"))
             t["w", i, g] = w
 
-        def mx_second(i, g):
+        def mx_second(i, g, engine):
             e = i // PER_FLOW
             bank = psum.tile([P, 512], F32, name="o_bank", tag="o_bank%d" % g)
             codes, scales = t["h_mx", i]
@@ -220,9 +259,9 @@ def tile_grouped_sylvester_step_k7_kernel(
             )
             t["o", i, g] = bank
 
-        def add(i, g):
+        def add(i, g, engine):
             if ("y", i) not in t:
-                t["y", i] = work.tile([P, D], F32, name="y", tag="y", bufs=4)
+                t["y", i] = work.tile([P, D], F32, name="y", tag="y", bufs=depth("add", "cast") + 1)
             nc.vector.tensor_tensor(
                 out=t["y", i][:, 512 * g : 512 * (g + 1)],
                 in0=t["o", i, g][:],
@@ -233,69 +272,62 @@ def tile_grouped_sylvester_step_k7_kernel(
             if t["added", i] == 2:
                 nc.sync.dma_start(out=y_rows[P * i : P * (i + 1), :], in_=t["y", i][:])
 
-        def cast_operands(i, g):
-            y_b = work.tile([P, 2, P, 2], BF16, name="y_b", tag="y_b%d" % g)
+        def cast(i, g, engine):
+            y_b = work.tile([P, 2, P, 2], BF16, name="y_b", tag="y_b%d" % g, bufs=depth("cast", "yT"))
+            src = t["y", i][:, 512 * g : 512 * (g + 1)].rearrange("r (p h e) -> r h p e", h=2, e=2)
+            if engine == "gpsimd":
+                nc.gpsimd.tensor_scalar(out=y_b[:], in0=src, scalar1=1.0, scalar2=0.0, op0=ALU.mult, op1=ALU.add)
+            else:
+                copy(engine, y_b[:], src)
             t["y_b", i, g] = y_b
-            return y_b[:], t["y", i][:, 512 * g : 512 * (g + 1)].rearrange("r (p h e) -> r h p e", h=2, e=2)
 
-        def cast_vector(i, g):
-            dst, src = cast_operands(i, g)
-            nc.vector.tensor_copy(out=dst, in_=src)
-
-        def cast_scalar(i, g):
-            dst, src = cast_operands(i, g)
-            nc.scalar.copy(out=dst, in_=src)
-
-        def cast_gpsimd(i, g):
-            dst, src = cast_operands(i, g)
-            nc.gpsimd.tensor_scalar(out=dst, in0=src, scalar1=1.0, scalar2=0.0, op0=ALU.mult, op1=ALU.add)
-
-        def y_turn(i, g):
+        def y_turn(i, g, engine):
             bank = psum.tile([P, 4, P], F32, name="y_bank", tag="y_bank")
             for j in range(4):
                 words = t["y_b", i, j // 2][:].rearrange("r h p e -> r (h p e)").bitcast(F32)
                 nc.tensor.transpose(bank[:, j, :], words[:, P * (j % 2) : P * (j % 2 + 1)], ident[:])
             t["y_bank", i] = bank
 
-        def y_copy(i, copy):
-            y_t = work.tile([P, D], BF16, name="y_t", tag="y_t", align_bytes=64, bufs=4)
+        def y_copy(i, g, engine):
+            if i % 2 == 0:
+                t["y_t", i // 2] = work.tile(
+                    [P, 2, 2, 512], BF16, name="y_t", tag="y_t", align_bytes=64, bufs=depth("ycopy", "yq", 2)
+                )
             copy(
-                out=y_t[:].bitcast(F32).rearrange("p (g r h) -> p g r h", g=2, h=2),
-                in_=t["y_bank", i][:].rearrange("p (g h) r -> p g r h", g=2),
+                engine,
+                t["y_t", i // 2][:, :, i % 2, :].bitcast(F32).rearrange("p g (r h) -> p g r h", h=2),
+                t["y_bank", i][:].rearrange("p (g h) r -> p g r h", g=2),
             )
-            t["y_t", i] = y_t
 
-        def y_quantise(i, g):
-            e, r0 = i // PER_FLOW, P * (i % PER_FLOW)
-            if ("y_mx", e) not in t:
+        def y_quantise(i, unused, engine):
+            e, g, m0 = i // PER_FLOW, i % 2, 2 * P * (i // 2)
+            r0 = m0 % R
+            if i % PER_FLOW == 0:
                 codes = work.tile([P, 2, R], U32, name="y_codes", tag="y_codes", align_bytes=64, bufs=2)
                 scales = work.tile([P, 2, R], U8, name="y_scales", tag="y_scales", align_bytes=64, bufs=2)
                 t["y_mx", e] = (codes, scales)
             codes, scales = t["y_mx", e]
             nc.vector.quantize_mx(
-                out=codes[:, g, r0 : r0 + P].bitcast(FP8X4),
-                scales=scales[:, g, r0 : r0 + P],
-                in_=t["y_t", i][:, 512 * g : 512 * (g + 1)],
+                out=codes[:, g, r0 : r0 + 2 * P].bitcast(FP8X4),
+                scales=scales[:, g, r0 : r0 + 2 * P],
+                in_=t["y_t", i // 2][:, g].rearrange("p i c -> p (i c)"),
             )
-            t["made", i // 2] = t.get(("made", i // 2), 0) + 1
-            if t["made", i // 2] == 4:
-                m0 = 2 * P * (i // 2)
-                nc.sync.dma_start(
-                    out=out_1[:, :, m0 : m0 + 2 * P, :].rearrange("g p m t -> p g (m t)").bitcast(I32),
-                    in_=codes[:, :, m0 % R : m0 % R + 2 * P].bitcast(I32),
-                )
-                if (i // 2) % 2 == 1:
-                    for q in range(4):
-                        nc.sync.dma_start(
-                            out=out_2[:, 4 * q : 4 * q + 4, R * e : R * (e + 1)].rearrange("g q m -> q g m").bitcast(I32),
-                            in_=scales[32 * q : 32 * q + 4, :, :].bitcast(I32),
-                        )
+            nc.sync.dma_start(
+                out=out_1[g, :, m0 : m0 + 2 * P, :].rearrange("p m t -> p (m t)").bitcast(I32),
+                in_=codes[:, g, r0 : r0 + 2 * P].bitcast(I32),
+            )
+            if i % PER_FLOW == PER_FLOW - 1:
+                for q in range(4):
+                    nc.sync.dma_start(
+                        out=out_2[:, 4 * q : 4 * q + 4, R * e : R * (e + 1)].rearrange("g q m -> q g m").bitcast(I32),
+                        in_=scales[32 * q : 32 * q + 4, :, :].bitcast(I32),
+                    )
 
         stage = {
             "zT": z_turn,
-            "zcopy": lambda i, g: z_copy(i, nc.scalar.copy),
-            "zcopyV": lambda i, g: z_copy(i, nc.vector.tensor_copy),
+            "zcopy": z_copy,
             "zq": z_quantise,
+            "wT": w_make,
             "mx1": mx_first,
             "tanh": tanh,
             "hT": h_turn,
@@ -305,21 +337,12 @@ def tile_grouped_sylvester_step_k7_kernel(
             "wcopy": w_copy,
             "mx2": mx_second,
             "add": add,
-            "castV": cast_vector,
-            "castA": cast_scalar,
-            "castP": cast_gpsimd,
+            "cast": cast,
             "yT": y_turn,
-            "ycopy": lambda i, g: y_copy(i, nc.scalar.copy),
-            "ycopyV": lambda i, g: y_copy(i, nc.vector.tensor_copy),
+            "ycopy": y_copy,
             "yq": y_quantise,
         }
-        pair_stage = {"wTV": w_vector, "wTA": w_scalar, "wTP": w_gpsimd}
-        lags = [lag for name, lag, g in STEP]
-        for s in range(min(lags), TILES + max(lags)):
-            for name, lag, g in STEP:
-                i = s - lag
-                if 0 <= i < TILES:
-                    if name in pair_stage:
-                        pair_stage[name](i // 2, g[i % 2])
-                    else:
-                        stage[name](i, g)
+        for s in range(TILES + max(lag for name, engine, lag, g in STEP)):
+            for name, engine, lag, g in STEP:
+                if 0 <= s - lag < TILES:
+                    stage[name](s - lag, g, engine)

@@ -23,31 +23,29 @@ U_ROW, C_ROW, D_ROW, ROWS = 0, 8, 16, 20
 
 GROUP = 2
 STEP = [
-    ("mx1", "tensor", 2, 0),
-    ("wT", "scalar", 3, (5, 2)),
-    ("wT", "gpsimd", 5, (1, 3)),
-    ("zT", "tensor", 0, 0),
-    ("wT", "gpsimd", 3, (0, 4)),
-    ("wTr", "tensor", 6, 0),
-    ("tanh", "scalar", 2, 0),
-    ("cast", "gpsimd", 7, 1),
-    ("hq", "vector", 4, 0),
-    ("wTr", "tensor", 5, 1),
-    ("hT", "tensor", 3, 0),
-    ("zcopy", "scalar", 0, 0),
-    ("yT", "tensor", 8, 0),
-    ("mx2", "tensor", 6, 0),
-    ("mx2", "tensor", 5, 1),
-    ("wcopy", "scalar", 6, 0),
-    ("wcopy", "scalar", 5, 1),
-    ("dmul", "vector", 3, 0),
-    ("add", "vector", 6, 0),
-    ("ycopy", "scalar", 8, 0),
-    ("add", "vector", 5, 1),
-    ("cast", "vector", 6, 0),
-    ("wT", "gpsimd", 3, (6, 7)),
-    ("zq", "vector", 0, 0),
-    ("yq", "vector", 11, 0),
+    ("zT", "T" * 16, 0, 0),
+    ("hT", "T" * 16, 6, 0),
+    ("tanh", "S" * 16, 5, 0),
+    ("perm", "V" * 16, 3, (2, 0, 1, 3)),
+    ("hq", "V" * 16, 7, 0),
+    ("zcopy", "S" * 16, 0, 0),
+    ("yT", "T" * 16, 12, 1),
+    ("dmul", "V" * 16, 6, 0),
+    ("wT", "S" * 16, 2, (7, 1)),
+    ("ycopy", "S" * 16, 12, 1),
+    ("yT", "T" * 16, 11, 0),
+    ("mx2", "T" * 16, 9, (0, 2)),
+    ("add", "V" * 16, 9, (0, 2)),
+    ("ycopy", "S" * 16, 11, 0),
+    ("mx2", "T" * 16, 9, (1, 3)),
+    ("wT", "V" + "G" * 9 + "S" * 6, 5, (3, 5)),
+    ("zq", "V" * 16, 0, 0),
+    ("add", "V" * 16, 9, (1, 3)),
+    ("cast", "G" * 12 + "V" * 4, 11, 0),
+    ("yq", "V" * 16, 12, 0),
+    ("wT", "V" * 4 + "S" * 12, 1, (2, 0)),
+    ("mx1", "T" * 16, 4, 0),
+    ("wT", "G" * 4 + "S" * 12, 4, (6, 4)),
 ]
 
 
@@ -73,15 +71,17 @@ def tile_grouped_sylvester_step_k7_kernel(
         ident = keep.tile([P, P], F32, name="ident")
         par_rows = keep.tile([P, 512], BF16, name="par_rows")
         par = keep.tile([P, ROWS, 4], F32, name="par")
-        warm = keep.tile([P, 8], F32, name="warm")
         b_plane = keep.tile([P, 2 * G, F], U8, name="b_plane", align_bytes=64)
-        a_plane = keep.tile([P, G, D], U8, name="a_plane", align_bytes=64)
-        z_raw = [keep.tile([P, D], BF16, name="z_raw%d" % i, align_bytes=64) for i in range(TILES)]
+        a_rows = keep.tile([P, G, D], U8, name="a_rows", align_bytes=64)
+        a_plane = keep.tile([P, G, 8, P], U8, name="a_plane", align_bytes=64)
+        z_raw = [keep.tile([P, 2, D], BF16, name="z_raw%d" % j, align_bytes=64) for j in range(TILES // 2)]
         b_code = [keep.tile([P, 2, 2 * F], U8, name="b_code%d" % e, align_bytes=64) for e in range(G)]
-        a_code = [keep.tile([P, 2 * D], U8, name="a_code%d" % e, align_bytes=64) for e in range(G)]
+        a_raw = [keep.tile([P, 2 * D], U8, name="a_raw%d" % e, align_bytes=64) for e in range(G)]
+        a_code = [keep.tile([P, 8, 2 * P], U8, name="a_code%d" % e, align_bytes=64) for e in range(G)]
 
-        def load_z(i):
-            nc.sync.dma_start(out=z_raw[i][:], in_=z_rows[P * i : P * (i + 1), :])
+        def load_z(first, count):
+            rows = z_rows[P * first : P * (first + count), :].rearrange("(i r) k -> r i k", r=P)
+            nc.sync.dma_start(out=z_raw[first // 2][:, first % 2 : first % 2 + count, :], in_=rows)
 
         def load_b(e):
             nc.sync.dma_start(
@@ -90,7 +90,7 @@ def tile_grouped_sylvester_step_k7_kernel(
             )
 
         def load_a(e):
-            nc.sync.dma_start(out=a_code[e][:].bitcast(I32), in_=a_words[e].bitcast(I32))
+            nc.sync.dma_start(out=a_raw[e][:].bitcast(I32), in_=a_words[e].bitcast(I32))
 
         def load_plane(queue, plane, rows, first, last):
             for q in range(4):
@@ -100,31 +100,28 @@ def tile_grouped_sylvester_step_k7_kernel(
                 )
 
         make_identity(nc, ident[:])
-        nc.vector.memset(b_plane[:, 0:2, :].bitcast(I32), 0)
         nc.vector.memset(par_rows[:], 0.0)
-        nc.vector.memset(a_plane[:, 0:1, :].bitcast(I32), 0)
-        nc.vector.memset(b_plane[:, 2:, :].bitcast(I32), 0)
-        nc.vector.memset(a_plane[:, 1:, :].bitcast(I32), 0)
-        load_z(0)
-        load_plane(nc.scalar, b_plane, b_scales, 0, 2)
-        nc.scalar.activation(out=warm[:], in_=ident[:, 0:8], func=ACT.Tanh)
-        load_b(0)
-        load_z(1)
+        nc.vector.memset(a_rows[:].bitcast(I32), 0)
+        nc.vector.memset(b_plane[:].bitcast(I32), 0)
+        load_z(0, 1)
+        load_z(1, 1)
         nc.sync.dma_start(out=par_rows[U_ROW:C_ROW, :], in_=u.rearrange("e (g k) -> (e g) k", g=2))
         nc.sync.dma_start(out=par_rows[C_ROW:D_ROW, :], in_=c.rearrange("e (g k) -> (e g) k", g=2))
         nc.sync.dma_start(out=par_rows[D_ROW:ROWS, :], in_=d)
-        load_z(2)
-        load_plane(nc.sync, a_plane, a_scales, 0, 1)
+        load_z(2, 2)
+        load_z(4, 2)
         load_a(0)
-        load_z(3)
-        load_z(4)
+        load_b(0)
+        load_plane(nc.sync, a_rows, a_scales, 0, 1)
+        load_plane(nc.sync, b_plane, b_scales, 0, 2)
+        load_z(6, 2)
+        load_plane(nc.sync, a_rows, a_scales, 1, G)
         load_plane(nc.sync, b_plane, b_scales, 2, 2 * G)
-        load_plane(nc.sync, a_plane, a_scales, 1, G)
         for e in range(1, G):
-            load_b(e)
             load_a(e)
-            for i in range(PER_FLOW * e + 1, min(PER_FLOW * (e + 1) + 1, TILES)):
-                load_z(i)
+            load_b(e)
+            for i in range(PER_FLOW * (e + 1), min(PER_FLOW * (e + 2), TILES), 2):
+                load_z(i, 2)
 
         t = {}
 
@@ -137,8 +134,8 @@ def tile_grouped_sylvester_step_k7_kernel(
             nc.vector.tensor_copy(out=par[:].rearrange("p j (h e) -> p j h e", e=2), in_=pairs[:, 0:ROWS])
 
         def z_turn(i, g, engine):
-            bank = psum.tile([P, 4, P], F32, name="z_bank", tag="z_bank")
-            words = z_raw[i][:].bitcast(F32)
+            bank = psum.tile([P, 4, P], F32, name="z_bank", tag="z_bank", bufs=2)
+            words = z_raw[i // 2][:, i % 2, :].bitcast(F32)
             for j in range(4):
                 first = 256 * (j // 2) + j % 2
                 nc.tensor.transpose(bank[:, j, :], words[:, first : 256 * (j // 2 + 1) : 2], ident[:])
@@ -147,7 +144,7 @@ def tile_grouped_sylvester_step_k7_kernel(
                 spread_parameters()
 
         def copy(engine, out, in_):
-            if engine == "scalar":
+            if engine == "S":
                 nc.scalar.copy(out=out, in_=in_)
             else:
                 nc.vector.tensor_copy(out=out, in_=in_)
@@ -177,17 +174,17 @@ def tile_grouped_sylvester_step_k7_kernel(
             group, j = i // GROUP, js[i % GROUP]
             if ("w_t", group, j // 4) not in t:
                 t["w_t", group, j // 4] = work.tile(
-                    [P, 4, GROUP, P], F32, name="w_t", tag="w_t%d" % (j // 4), bufs=depth("wT", "wTr", GROUP)
+                    [P, 4, GROUP, P], F32, name="w_t", tag="w_t%d" % (j // 4), bufs=depth("wT", "add", GROUP)
                 )
             row = 2 * (i // PER_FLOW) + j // 4
             dst = t["w_t", group, j // 4][:, j % 4]
             src = t["z_t", group][:].rearrange("p i (g r t) -> p g t i r", g=2, t=4)[:, j // 4, j % 4]
             scale = par[:, U_ROW + row, j % 4 : j % 4 + 1]
             shift = par[:, C_ROW + row, j % 4 : j % 4 + 1]
-            if engine == "scalar":
+            if engine == "S":
                 nc.scalar.activation(out=dst, in_=src, func=ACT.Identity, bias=shift, scale=scale)
             else:
-                unit = nc.vector if engine == "vector" else nc.gpsimd
+                unit = nc.vector if engine == "V" else nc.gpsimd
                 unit.tensor_scalar(out=dst, in0=src, scalar1=scale, scalar2=shift, op0=ALU.mult, op1=ALU.add)
 
         def mx_first(i, g, engine):
@@ -226,81 +223,85 @@ def tile_grouped_sylvester_step_k7_kernel(
             t["h_t", i] = h_t
 
         def h_quantise(i, g, engine):
-            codes = work.tile([P, P], U32, name="h_codes", tag="h_codes", align_bytes=64, bufs=depth("hq", "mx2"))
-            scales = work.tile([P, P], U8, name="h_scales", tag="h_scales", align_bytes=64, bufs=depth("hq", "mx2"))
+            if i % 2 == 0:
+                bufs = depth("hq", "mx2", 2)
+                codes = work.tile([P, 2 * P], U32, name="h_codes", tag="h_codes", align_bytes=64, bufs=bufs)
+                scales = work.tile([P, 2 * P], U8, name="h_scales", tag="h_scales", align_bytes=64, bufs=bufs)
+                t["h_mx", i // 2] = (codes, scales)
+            codes, scales = t["h_mx", i // 2]
+            cols = slice(P * (i % 2), P * (i % 2 + 1))
             nc.vector.quantize_mx(
-                out=codes[:].bitcast(FP8X4), scales=scales[:], in_=t["h_t", i][:].rearrange("p r t -> p (r t)")
+                out=codes[:, cols].bitcast(FP8X4),
+                scales=scales[:, cols],
+                in_=t["h_t", i][:].rearrange("p r t -> p (r t)"),
             )
-            t["h_mx", i] = (codes, scales)
 
-        def w_turn(i, g, engine):
-            bank = psum.tile([P, 4, P], F32, name="w_bank", tag="w_bank%d" % g)
-            for j in range(4):
-                nc.tensor.transpose(bank[:, j, :], t["w_t", i // GROUP, g][:, j, i % GROUP, :], ident[:])
-            t["w_bank", i, g] = bank
-
-        def w_copy(i, g, engine):
-            w = work.tile([P, P, 4], F32, name="w", tag="w%d" % g, bufs=depth("wcopy", "add"))
-            copy(engine, w[:], t["w_bank", i, g][:].rearrange("r t m -> r m t"))
-            t["w", i, g] = w
-
-        def mx_second(i, g, engine):
-            e = i // PER_FLOW
-            bank = psum.tile([P, 512], F32, name="o_bank", tag="o_bank%d" % g)
-            codes, scales = t["h_mx", i]
-            nc.tensor.matmul_mx(
-                out=bank[:],
-                lhsT=codes[:].bitcast(FP8X4),
-                lhsT_scale=scales[:],
-                rhs=a_code[e][:, 1024 * g : 1024 * (g + 1)].bitcast(FP4X4),
-                rhs_scale=a_plane[:, e, 512 * g : 512 * (g + 1)],
-                start=True,
-                stop=True,
+        def a_order(i, quarters, engine):
+            e, b = i // PER_FLOW, quarters[i % PER_FLOW]
+            g, t0 = b // 2, 2 * (b % 2)
+            nc.vector.tensor_copy(
+                out=a_code[e][:, 2 * b : 2 * b + 2, :].rearrange("p t (m y) -> p t m y", y=2),
+                in_=a_raw[e][:].rearrange("p (g m t y) -> p g t m y", g=2, t=4, y=2)[:, g, t0 : t0 + 2],
             )
-            t["o", i, g] = bank
+            nc.vector.tensor_copy(
+                out=a_plane[:, e, 2 * b : 2 * b + 2, :],
+                in_=a_rows[:, e, :].rearrange("p (g m t) -> p g t m", g=2, t=4)[:, g, t0 : t0 + 2],
+            )
 
-        def add(i, g, engine):
-            if ("y", i) not in t:
-                t["y", i] = work.tile([P, D], F32, name="y", tag="y", bufs=depth("add", "cast") + 1)
+        def mx_second(i, quarters, engine):
+            e, b = i // PER_FLOW, quarters[i % 2]
+            bank = psum.tile([P, 2, 2 * P], F32, name="o_bank", tag="o_bank", bufs=2)
+            codes, scales = t["h_mx", i // 2]
+            for j in range(2):
+                nc.tensor.matmul_mx(
+                    out=bank[:, j, :],
+                    lhsT=a_code[e][:, 2 * b + j, :].bitcast(FP4X4),
+                    lhsT_scale=a_plane[:, e, 2 * b + j, :],
+                    rhs=codes[:].bitcast(FP8X4),
+                    rhs_scale=scales[:],
+                    start=True,
+                    stop=True,
+                )
+            t["o", i // 2, b] = bank
+
+        def add(i, quarters, engine):
+            pair, b = i // 2, quarters[i % 2]
+            g, t0 = b // 2, 2 * (b % 2)
+            if ("y_t", pair, g) not in t:
+                bufs = max(depth("add", "cast", 2), depth("add", "yT", 2))
+                t["y_t", pair, g] = work.tile([P, 4, 2 * P], F32, name="y_t", tag="y_t%d" % g, bufs=bufs)
             nc.vector.tensor_tensor(
-                out=t["y", i][:, 512 * g : 512 * (g + 1)],
-                in0=t["o", i, g][:],
-                in1=t["w", i, g][:].rearrange("r m t -> r (m t)"),
+                out=t["y_t", pair, g][:, t0 : t0 + 2, :],
+                in0=t["o", pair, b][:],
+                in1=t["w_t", pair, g][:, t0 : t0 + 2].rearrange("p t i r -> p t (i r)"),
                 op=ALU.add,
             )
-            t["added", i] = t.get(("added", i), 0) + 1
-            if t["added", i] == 2:
-                nc.sync.dma_start(out=y_rows[P * i : P * (i + 1), :], in_=t["y", i][:])
 
-        def cast(i, g, engine):
-            y_b = work.tile([P, 2, P, 2], BF16, name="y_b", tag="y_b%d" % g, bufs=depth("cast", "yT"))
-            src = t["y", i][:, 512 * g : 512 * (g + 1)].rearrange("r (p h e) -> r h p e", h=2, e=2)
-            if engine == "gpsimd":
+        def cast(i, flip, engine):
+            pair, g = i // 2, (i + flip) % 2
+            y_b = work.tile([P, 2 * P, 4], BF16, name="y_b", tag="y_b", align_bytes=64, bufs=depth("cast", "yq"))
+            src = t["y_t", pair, g][:].rearrange("p t r -> p r t")
+            if engine == "G":
                 nc.gpsimd.tensor_scalar(out=y_b[:], in0=src, scalar1=1.0, scalar2=0.0, op0=ALU.mult, op1=ALU.add)
             else:
                 copy(engine, y_b[:], src)
-            t["y_b", i, g] = y_b
+            t["y_b", pair, g] = y_b
 
         def y_turn(i, g, engine):
-            bank = psum.tile([P, 4, P], F32, name="y_bank", tag="y_bank")
+            bank = psum.tile([P, 4, P], F32, name="y_bank", tag="y_bank%d" % g)
             for j in range(4):
-                words = t["y_b", i, j // 2][:].rearrange("r h p e -> r (h p e)").bitcast(F32)
-                nc.tensor.transpose(bank[:, j, :], words[:, P * (j % 2) : P * (j % 2 + 1)], ident[:])
-            t["y_bank", i] = bank
+                nc.tensor.transpose(bank[:, j, :], t["y_t", i // 2, g][:, j, P * (i % 2) : P * (i % 2 + 1)], ident[:])
+            t["y_bank", i, g] = bank
 
         def y_copy(i, g, engine):
-            if i % 2 == 0:
-                t["y_t", i // 2] = work.tile(
-                    [P, 2, 2, 512], BF16, name="y_t", tag="y_t", align_bytes=64, bufs=depth("ycopy", "yq", 2)
-                )
-            copy(
-                engine,
-                t["y_t", i // 2][:, :, i % 2, :].bitcast(F32).rearrange("p g (r h) -> p g r h", h=2),
-                t["y_bank", i][:].rearrange("p (g h) r -> p g r h", g=2),
+            y = work.tile([P, P, 4], F32, name="y", tag="y", bufs=8)
+            copy(engine, y[:], t["y_bank", i, g][:].rearrange("r t m -> r m t"))
+            nc.sync.dma_start(
+                out=y_rows[P * i : P * (i + 1), 512 * g : 512 * (g + 1)], in_=y[:].rearrange("r m t -> r (m t)")
             )
 
-        def y_quantise(i, unused, engine):
-            e, g, m0 = i // PER_FLOW, i % 2, 2 * P * (i // 2)
+        def y_quantise(i, flip, engine):
+            e, g, m0 = i // PER_FLOW, (i + flip) % 2, 2 * P * (i // 2)
             r0 = m0 % R
             if i % PER_FLOW == 0:
                 codes = work.tile([P, 2, R], U32, name="y_codes", tag="y_codes", align_bytes=64, bufs=2)
@@ -310,15 +311,16 @@ def tile_grouped_sylvester_step_k7_kernel(
             nc.vector.quantize_mx(
                 out=codes[:, g, r0 : r0 + 2 * P].bitcast(FP8X4),
                 scales=scales[:, g, r0 : r0 + 2 * P],
-                in_=t["y_t", i // 2][:, g].rearrange("p i c -> p (i c)"),
+                in_=t["y_b", i // 2, g][:].rearrange("p r t -> p (r t)"),
             )
             nc.sync.dma_start(
                 out=out_1[g, :, m0 : m0 + 2 * P, :].rearrange("p m t -> p (m t)").bitcast(I32),
                 in_=codes[:, g, r0 : r0 + 2 * P].bitcast(I32),
             )
             if i % PER_FLOW == PER_FLOW - 1:
+                queue = nc.scalar if i == TILES - 1 else nc.sync
                 for q in range(4):
-                    nc.sync.dma_start(
+                    queue.dma_start(
                         out=out_2[:, 4 * q : 4 * q + 4, R * e : R * (e + 1)].rearrange("g q m -> q g m").bitcast(I32),
                         in_=scales[32 * q : 32 * q + 4, :, :].bitcast(I32),
                     )
@@ -333,8 +335,7 @@ def tile_grouped_sylvester_step_k7_kernel(
             "hT": h_turn,
             "dmul": h_scale,
             "hq": h_quantise,
-            "wTr": w_turn,
-            "wcopy": w_copy,
+            "perm": a_order,
             "mx2": mx_second,
             "add": add,
             "cast": cast,
@@ -345,4 +346,4 @@ def tile_grouped_sylvester_step_k7_kernel(
         for s in range(TILES + max(lag for name, engine, lag, g in STEP)):
             for name, engine, lag, g in STEP:
                 if 0 <= s - lag < TILES:
-                    stage[name](s - lag, g, engine)
+                    stage[name](s - lag, g, engine[s - lag])

from contextlib import ExitStack

import concourse.mybir as mybir
from concourse.masks import make_identity

G, R, D, F = 4, 512, 1024, 512
FLOPS = 2 * G * R * D * F * 2

F32 = mybir.dt.float32
BF16 = mybir.dt.bfloat16
I32 = mybir.dt.int32
U32 = mybir.dt.uint32
U8 = mybir.dt.uint8
FP8X4 = mybir.dt.float8_e4m3fn_x4
FP4X4 = mybir.dt.float4_e2m1fn_x4
ACT = mybir.ActivationFunctionType
ALU = mybir.AluOpType

P = 128
TILES = G * R // P
PER_FLOW = R // P
U_ROW, C_ROW, D_ROW, ROWS = 0, 8, 16, 20

GROUP = 2
STEP = [
    ("zT", "T" * 16, 0, 0),
    ("hT", "T" * 16, 6, 0),
    ("tanh", "S" * 16, 5, 0),
    ("perm", "V" * 16, 3, (2, 0, 1, 3)),
    ("hq", "V" * 16, 7, 0),
    ("zcopy", "S" * 16, 0, 0),
    ("yT", "T" * 16, 12, 1),
    ("dmul", "V" * 16, 6, 0),
    ("wT", "S" * 16, 2, (7, 1)),
    ("ycopy", "S" * 16, 12, 1),
    ("yT", "T" * 16, 11, 0),
    ("mx2", "T" * 16, 9, (0, 2)),
    ("add", "V" * 16, 9, (0, 2)),
    ("ycopy", "S" * 16, 11, 0),
    ("mx2", "T" * 16, 9, (1, 3)),
    ("wT", "V" + "G" * 9 + "S" * 6, 5, (3, 5)),
    ("zq", "V" * 16, 0, 0),
    ("add", "V" * 16, 9, (1, 3)),
    ("cast", "G" * 12 + "V" * 4, 11, 0),
    ("yq", "V" * 16, 12, 0),
    ("wT", "V" * 4 + "S" * 12, 1, (2, 0)),
    ("mx1", "T" * 16, 4, 0),
    ("wT", "G" * 4 + "S" * 12, 4, (6, 4)),
]


def depth(first, last, per=1):
    lags_first = [lag for name, engine, lag, g in STEP if name == first]
    lags_last = [lag for name, engine, lag, g in STEP if name == last]
    return (max(lags_last) - min(lags_first) + per) // per + 2


def tile_grouped_sylvester_step_k7_kernel(
    tc, z, u, d, c, b_words, b_scales, a_words, a_scales, out_0, out_1, out_2
):
    nc = tc.nc
    z_rows = z.rearrange("e r k -> (e r) k")
    y_rows = out_0.rearrange("e r k -> (e r) k")

    with ExitStack() as ctx:
        keep = ctx.enter_context(tc.tile_pool(name="keep", bufs=1))
        work = ctx.enter_context(tc.tile_pool(name="work", bufs=3))
        psum = ctx.enter_context(tc.psum_pool(name="psum", bufs=1))
        ctx.enter_context(tc.manual_schedule())

        ident = keep.tile([P, P], F32, name="ident")
        par_rows = keep.tile([P, 512], BF16, name="par_rows")
        par = keep.tile([P, ROWS, 4], F32, name="par")
        b_plane = keep.tile([P, 2 * G, F], U8, name="b_plane", align_bytes=64)
        a_rows = keep.tile([P, G, D], U8, name="a_rows", align_bytes=64)
        a_plane = keep.tile([P, G, 8, P], U8, name="a_plane", align_bytes=64)
        z_raw = [keep.tile([P, 2, D], BF16, name="z_raw%d" % j, align_bytes=64) for j in range(TILES // 2)]
        b_code = [keep.tile([P, 2, 2 * F], U8, name="b_code%d" % e, align_bytes=64) for e in range(G)]
        a_raw = [keep.tile([P, 2 * D], U8, name="a_raw%d" % e, align_bytes=64) for e in range(G)]
        a_code = [keep.tile([P, 8, 2 * P], U8, name="a_code%d" % e, align_bytes=64) for e in range(G)]

        def load_z(first, count):
            rows = z_rows[P * first : P * (first + count), :].rearrange("(i r) k -> r i k", r=P)
            nc.sync.dma_start(out=z_raw[first // 2][:, first % 2 : first % 2 + count, :], in_=rows)

        def load_b(e):
            nc.sync.dma_start(
                out=b_code[e][:].bitcast(I32),
                in_=b_words[2 * e : 2 * e + 2].rearrange("g p n -> p g n").bitcast(I32),
            )

        def load_a(e):
            nc.sync.dma_start(out=a_raw[e][:].bitcast(I32), in_=a_words[e].bitcast(I32))

        def load_plane(queue, plane, rows, first, last):
            for q in range(4):
                queue.dma_start(
                    out=plane[32 * q : 32 * q + 4, first:last, :].bitcast(I32),
                    in_=rows[first:last, 4 * q : 4 * q + 4, :].rearrange("g r n -> r g n").bitcast(I32),
                )

        make_identity(nc, ident[:])
        nc.vector.memset(par_rows[:], 0.0)
        nc.vector.memset(a_rows[:].bitcast(I32), 0)
        nc.vector.memset(b_plane[:].bitcast(I32), 0)
        load_z(0, 1)
        load_z(1, 1)
        nc.sync.dma_start(out=par_rows[U_ROW:C_ROW, :], in_=u.rearrange("e (g k) -> (e g) k", g=2))
        nc.sync.dma_start(out=par_rows[C_ROW:D_ROW, :], in_=c.rearrange("e (g k) -> (e g) k", g=2))
        nc.sync.dma_start(out=par_rows[D_ROW:ROWS, :], in_=d)
        load_z(2, 2)
        load_z(4, 2)
        load_a(0)
        load_b(0)
        load_plane(nc.sync, a_rows, a_scales, 0, 1)
        load_plane(nc.sync, b_plane, b_scales, 0, 2)
        load_z(6, 2)
        load_plane(nc.sync, a_rows, a_scales, 1, G)
        load_plane(nc.sync, b_plane, b_scales, 2, 2 * G)
        for e in range(1, G):
            load_a(e)
            load_b(e)
            for i in range(PER_FLOW * (e + 1), min(PER_FLOW * (e + 2), TILES), 2):
                load_z(i, 2)

        t = {}

        def spread_parameters():
            bank = psum.tile([P, 4, P], F32, name="par_bank", tag="h_bank")
            words = par_rows[:].bitcast(F32)
            for half in range(2):
                nc.tensor.transpose(bank[:, half, :], words[:, half:256:2], ident[:])
            pairs = bank[:, 0:2, :].bitcast(BF16).rearrange("p h (j e) -> p j h e", e=2)
            nc.vector.tensor_copy(out=par[:].rearrange("p j (h e) -> p j h e", e=2), in_=pairs[:, 0:ROWS])

        def z_turn(i, g, engine):
            bank = psum.tile([P, 4, P], F32, name="z_bank", tag="z_bank", bufs=2)
            words = z_raw[i // 2][:, i % 2, :].bitcast(F32)
            for j in range(4):
                first = 256 * (j // 2) + j % 2
                nc.tensor.transpose(bank[:, j, :], words[:, first : 256 * (j // 2 + 1) : 2], ident[:])
            t["z_bank", i] = bank
            if i == 1:
                spread_parameters()

        def copy(engine, out, in_):
            if engine == "S":
                nc.scalar.copy(out=out, in_=in_)
            else:
                nc.vector.tensor_copy(out=out, in_=in_)

        def z_copy(i, g, engine):
            if i % GROUP == 0:
                t["z_t", i // GROUP] = work.tile(
                    [P, GROUP, D], BF16, name="z_t", tag="z_t", align_bytes=64,
                    bufs=max(depth("zcopy", "wT", GROUP), depth("zcopy", "zq", GROUP)),
                )
            copy(
                engine,
                t["z_t", i // GROUP][:, i % GROUP, :].bitcast(F32).rearrange("p (g r h) -> p g r h", g=2, h=2),
                t["z_bank", i][:].rearrange("p (g h) r -> p g r h", g=2),
            )

        def z_quantise(i, g, engine):
            bufs = depth("zq", "mx1")
            codes = work.tile([P, 2 * P], U32, name="z_codes", tag="z_codes", align_bytes=64, bufs=bufs)
            scales = work.tile([P, 2 * P], U8, name="z_scales", tag="z_scales", align_bytes=64, bufs=bufs)
            nc.vector.quantize_mx(
                out=codes[:].bitcast(FP8X4), scales=scales[:], in_=t["z_t", i // GROUP][:, i % GROUP, :]
            )
            t["z_mx", i] = (codes, scales)

        def w_make(i, js, engine):
            group, j = i // GROUP, js[i % GROUP]
            if ("w_t", group, j // 4) not in t:
                t["w_t", group, j // 4] = work.tile(
                    [P, 4, GROUP, P], F32, name="w_t", tag="w_t%d" % (j // 4), bufs=depth("wT", "add", GROUP)
                )
            row = 2 * (i // PER_FLOW) + j // 4
            dst = t["w_t", group, j // 4][:, j % 4]
            src = t["z_t", group][:].rearrange("p i (g r t) -> p g t i r", g=2, t=4)[:, j // 4, j % 4]
            scale = par[:, U_ROW + row, j % 4 : j % 4 + 1]
            shift = par[:, C_ROW + row, j % 4 : j % 4 + 1]
            if engine == "S":
                nc.scalar.activation(out=dst, in_=src, func=ACT.Identity, bias=shift, scale=scale)
            else:
                unit = nc.vector if engine == "V" else nc.gpsimd
                unit.tensor_scalar(out=dst, in0=src, scalar1=scale, scalar2=shift, op0=ALU.mult, op1=ALU.add)

        def mx_first(i, g, engine):
            e = i // PER_FLOW
            bank = psum.tile([P, F], F32, name="pre_bank", tag="pre_bank")
            codes, scales = t["z_mx", i]
            for k in range(2):
                nc.tensor.matmul_mx(
                    out=bank[:],
                    lhsT=codes[:, P * k : P * (k + 1)].bitcast(FP8X4),
                    lhsT_scale=scales[:, P * k : P * (k + 1)],
                    rhs=b_code[e][:, k, :].bitcast(FP4X4),
                    rhs_scale=b_plane[:, 2 * e + k, :],
                    start=(k == 0),
                    stop=(k == 1),
                )
            t["pre", i] = bank

        def tanh(i, g, engine):
            th = work.tile([P, 4, P], F32, name="th", tag="th", bufs=depth("tanh", "hT"))
            nc.scalar.activation(out=th[:], in_=t["pre", i][:].rearrange("r (m t) -> r t m", t=4), func=ACT.Tanh)
            t["th", i] = th

        def h_turn(i, g, engine):
            bank = psum.tile([P, 4, P], F32, name="h_bank", tag="h_bank")
            for j in range(4):
                nc.tensor.transpose(bank[:, j, :], t["th", i][:, j, :], ident[:])
            t["h_bank", i] = bank

        def h_scale(i, g, engine):
            h_t = work.tile([P, P, 4], BF16, name="h_t", tag="h_t", align_bytes=64, bufs=depth("dmul", "hq"))
            gain = par[:, D_ROW + i // PER_FLOW, :].unsqueeze(1).to_broadcast([P, P, 4])
            nc.vector.tensor_tensor(
                out=h_t[:], in0=t["h_bank", i][:].rearrange("p t r -> p r t"), in1=gain, op=ALU.mult
            )
            t["h_t", i] = h_t

        def h_quantise(i, g, engine):
            if i % 2 == 0:
                bufs = depth("hq", "mx2", 2)
                codes = work.tile([P, 2 * P], U32, name="h_codes", tag="h_codes", align_bytes=64, bufs=bufs)
                scales = work.tile([P, 2 * P], U8, name="h_scales", tag="h_scales", align_bytes=64, bufs=bufs)
                t["h_mx", i // 2] = (codes, scales)
            codes, scales = t["h_mx", i // 2]
            cols = slice(P * (i % 2), P * (i % 2 + 1))
            nc.vector.quantize_mx(
                out=codes[:, cols].bitcast(FP8X4),
                scales=scales[:, cols],
                in_=t["h_t", i][:].rearrange("p r t -> p (r t)"),
            )

        def a_order(i, quarters, engine):
            e, b = i // PER_FLOW, quarters[i % PER_FLOW]
            g, t0 = b // 2, 2 * (b % 2)
            nc.vector.tensor_copy(
                out=a_code[e][:, 2 * b : 2 * b + 2, :].rearrange("p t (m y) -> p t m y", y=2),
                in_=a_raw[e][:].rearrange("p (g m t y) -> p g t m y", g=2, t=4, y=2)[:, g, t0 : t0 + 2],
            )
            nc.vector.tensor_copy(
                out=a_plane[:, e, 2 * b : 2 * b + 2, :],
                in_=a_rows[:, e, :].rearrange("p (g m t) -> p g t m", g=2, t=4)[:, g, t0 : t0 + 2],
            )

        def mx_second(i, quarters, engine):
            e, b = i // PER_FLOW, quarters[i % 2]
            bank = psum.tile([P, 2, 2 * P], F32, name="o_bank", tag="o_bank", bufs=2)
            codes, scales = t["h_mx", i // 2]
            for j in range(2):
                nc.tensor.matmul_mx(
                    out=bank[:, j, :],
                    lhsT=a_code[e][:, 2 * b + j, :].bitcast(FP4X4),
                    lhsT_scale=a_plane[:, e, 2 * b + j, :],
                    rhs=codes[:].bitcast(FP8X4),
                    rhs_scale=scales[:],
                    start=True,
                    stop=True,
                )
            t["o", i // 2, b] = bank

        def add(i, quarters, engine):
            pair, b = i // 2, quarters[i % 2]
            g, t0 = b // 2, 2 * (b % 2)
            if ("y_t", pair, g) not in t:
                bufs = max(depth("add", "cast", 2), depth("add", "yT", 2))
                t["y_t", pair, g] = work.tile([P, 4, 2 * P], F32, name="y_t", tag="y_t%d" % g, bufs=bufs)
            nc.vector.tensor_tensor(
                out=t["y_t", pair, g][:, t0 : t0 + 2, :],
                in0=t["o", pair, b][:],
                in1=t["w_t", pair, g][:, t0 : t0 + 2].rearrange("p t i r -> p t (i r)"),
                op=ALU.add,
            )

        def cast(i, flip, engine):
            pair, g = i // 2, (i + flip) % 2
            y_b = work.tile([P, 2 * P, 4], BF16, name="y_b", tag="y_b", align_bytes=64, bufs=depth("cast", "yq"))
            src = t["y_t", pair, g][:].rearrange("p t r -> p r t")
            if engine == "G":
                nc.gpsimd.tensor_scalar(out=y_b[:], in0=src, scalar1=1.0, scalar2=0.0, op0=ALU.mult, op1=ALU.add)
            else:
                copy(engine, y_b[:], src)
            t["y_b", pair, g] = y_b

        def y_turn(i, g, engine):
            bank = psum.tile([P, 4, P], F32, name="y_bank", tag="y_bank%d" % g)
            for j in range(4):
                nc.tensor.transpose(bank[:, j, :], t["y_t", i // 2, g][:, j, P * (i % 2) : P * (i % 2 + 1)], ident[:])
            t["y_bank", i, g] = bank

        def y_copy(i, g, engine):
            y = work.tile([P, P, 4], F32, name="y", tag="y", bufs=8)
            copy(engine, y[:], t["y_bank", i, g][:].rearrange("r t m -> r m t"))
            nc.sync.dma_start(
                out=y_rows[P * i : P * (i + 1), 512 * g : 512 * (g + 1)], in_=y[:].rearrange("r m t -> r (m t)")
            )

        def y_quantise(i, flip, engine):
            e, g, m0 = i // PER_FLOW, (i + flip) % 2, 2 * P * (i // 2)
            r0 = m0 % R
            if i % PER_FLOW == 0:
                codes = work.tile([P, 2, R], U32, name="y_codes", tag="y_codes", align_bytes=64, bufs=2)
                scales = work.tile([P, 2, R], U8, name="y_scales", tag="y_scales", align_bytes=64, bufs=2)
                t["y_mx", e] = (codes, scales)
            codes, scales = t["y_mx", e]
            nc.vector.quantize_mx(
                out=codes[:, g, r0 : r0 + 2 * P].bitcast(FP8X4),
                scales=scales[:, g, r0 : r0 + 2 * P],
                in_=t["y_b", i // 2, g][:].rearrange("p r t -> p (r t)"),
            )
            nc.sync.dma_start(
                out=out_1[g, :, m0 : m0 + 2 * P, :].rearrange("p m t -> p (m t)").bitcast(I32),
                in_=codes[:, g, r0 : r0 + 2 * P].bitcast(I32),
            )
            if i % PER_FLOW == PER_FLOW - 1:
                queue = nc.scalar if i == TILES - 1 else nc.sync
                for q in range(4):
                    queue.dma_start(
                        out=out_2[:, 4 * q : 4 * q + 4, R * e : R * (e + 1)].rearrange("g q m -> q g m").bitcast(I32),
                        in_=scales[32 * q : 32 * q + 4, :, :].bitcast(I32),
                    )

        stage = {
            "zT": z_turn,
            "zcopy": z_copy,
            "zq": z_quantise,
            "wT": w_make,
            "mx1": mx_first,
            "tanh": tanh,
            "hT": h_turn,
            "dmul": h_scale,
            "hq": h_quantise,
            "perm": a_order,
            "mx2": mx_second,
            "add": add,
            "cast": cast,
            "yT": y_turn,
            "ycopy": y_copy,
            "yq": y_quantise,
        }
        for s in range(TILES + max(lag for name, engine, lag, g in STEP)):
            for name, engine, lag, g in STEP:
                if 0 <= s - lag < TILES:
                    stage[name](s - lag, g, engine[s - lag])
